import numpy as np
import ml_dtypes


def mxq(x, axis, fmt="e4m3"):
    dtype, down = {"e4m3": (ml_dtypes.float8_e4m3fn, 7), "e5m2": (ml_dtypes.float8_e5m2, 14)}[fmt]
    v = np.moveaxis(np.asarray(x, np.float32).astype(ml_dtypes.bfloat16).astype(np.float64), axis, -1)
    blocks = v.reshape(v.shape[:-1] + (-1, 32))
    amax = np.abs(blocks).max(-1, keepdims=True)
    byte = np.maximum(np.where(amax > 0, np.frexp(amax)[1] - 1 + 127, 0) - down, 1)
    scale = np.exp2(byte - 127.0)
    codes = (blocks / scale).astype(np.float32).astype(dtype).astype(np.float64)
    return np.moveaxis((codes * scale).reshape(v.shape), -1, axis)


WIDE = False


def mx_kscale(k):
    if not WIDE:
        return np.ones(k)
    levels = np.array([10, -10, 5, -5, 0])
    if k % 512:
        return np.exp2(np.random.permutation(np.resize(levels, k // 32))).repeat(32)
    a = np.empty((k // 512, 16))
    for p in range(k // 512):
        a[p, :8] = np.random.permutation(np.resize(levels, 8))
        for g in range(8):
            far = levels[np.abs(levels - a[p, g]) >= 10]
            a[p, g + 8] = far[np.random.randint(len(far))]
    return np.exp2(a.ravel()).repeat(32)


def f64(x):
    return np.asarray(x).astype(np.float64)


def striped(idx):
    return np.tile(idx.reshape(-1, 16).T, (8, 1)).astype(np.uint16)


def unstriped(offs):
    return offs[:16].T.reshape(-1).astype(np.int64)


def pack_weight(w):
    k, n = w.shape
    w = f64(np.asarray(w, np.float32).astype(ml_dtypes.bfloat16)).reshape(k // 32, 32, n)
    amax = np.abs(w).max(1)
    byte = np.clip(np.where(amax > 0, np.frexp(amax)[1] - 1 + 127 - 7, 1), 1, 254)
    scaled = (w * np.exp2(127.0 - byte)[:, None, :]).reshape(k, n).astype(np.float32)
    words = np.ascontiguousarray(scaled.reshape(k // 512, 128, 4, n).transpose(0, 1, 3, 2)).astype(ml_dtypes.float8_e4m3fn).view(np.uint8)
    return words, np.ascontiguousarray(byte.astype(np.uint8).reshape(k // 512, 16, n))


def unpack_weight(words, scales):
    g, p, n, _ = words.shape
    vals = np.ascontiguousarray(words).view(ml_dtypes.float8_e4m3fn).astype(np.float64) * np.repeat(np.exp2(scales.astype(np.float64) - 127.0), 8, axis=1)[..., None]
    return vals.transpose(0, 1, 3, 2).reshape(g * 512, n)


K, T, S, N, U = 1024, 2048, 512, 128, 512
P = 2 ** 7


def setup_inputs():
    n = np.random.standard_normal
    s = mx_kscale(K)[:, None]
    packed_xT = pack_weight(n((K, T)) * s)
    return {
        "x_words": packed_xT[0],
        "x_scales": packed_xT[1],
        "w1": (n((K, N)) / np.sqrt(K) / s).astype(np.float32),
        "w2": (n((K, N)) / np.sqrt(K) / s).astype(np.float32),
        "w3": (n((K, N)) / np.sqrt(K) / s).astype(np.float32),
        "logfk": (np.tile(np.random.uniform(0.1, 0.8, U) * np.where(np.random.uniform(size=U) < 0.5, 1.0, -1.0), (P, 1))).astype(np.float32),
        "mat": (np.tile(np.random.uniform(0.2, 2.0, U), (P, 1))).astype(np.float32),
        "offs": striped(np.random.permutation(T)[:S]),
        "expy": striped(np.random.randint(0, S, U)),
    }


def reference(x_words, x_scales, w1, w2, w3, logfk, mat, offs, expy):
    xq = unpack_weight(x_words, x_scales)[:, unstriped(offs)]
    ya = mxq(f64(w1), 0, "e4m3").T @ xq
    alp = 0.3 * (np.log(np.exp(ya) + 1.0) + 0.3)
    ag = alp[:, unstriped(expy)]
    yv = mxq(f64(w3), 0, "e4m3").T @ xq
    nu = 0.5 * (np.log(np.exp(yv) + 1.0)) + 0.1
    vg = nu[:, unstriped(expy)]
    zr = (vg * f64(logfk)[:1]) / ag
    yr = mxq(f64(w2), 0, "e4m3").T @ xq
    rho = 0.7 * np.tanh(yr)
    rg = rho[:, unstriped(expy)]
    xz = np.log((np.sqrt(-1.0 * (2.0 * (rg * zr)) + 1.0 + (zr) ** 2) + zr - rg) / (-1.0 * rg + 1.0))
    return 4.0 * (((ag * zr) / xz) * ((0.25 * ((rg * vg) * ag) + (((vg) ** 2) * (-3.0 * ((rg) ** 2) + 2.0)) / 24) * f64(mat)[:1] + 1.0))

@@ -1,0 +1,253 @@
+import math
+from contextlib import ExitStack
+
+import concourse.mybir as mybir
+
+K, T, S, N, U = 1024, 2048, 512, 128, 512
+FLOPS = 3 * 2 * K * N * S
+
+F32 = mybir.dt.float32
+BF16 = mybir.dt.bfloat16
+I32 = mybir.dt.int32
+U32 = mybir.dt.uint32
+U16 = mybir.dt.uint16
+U8 = mybir.dt.uint8
+FP8X4 = mybir.dt.float8_e4m3fn_x4
+ALU = mybir.AluOpType
+ACT = mybir.ActivationFunctionType
+
+P = 128
+PACK = 4
+PASSES = K // (P * PACK)
+HALF = U // 2
+EXP_CAP = 30.0
+
+
+def tile_picked_ysabr_vol_p_kernel(tc, x_words, x_scales, w1, w2, w3, logfk, mat, offs, expy, out):
+    nc = tc.nc
+    halves = [slice(h * HALF, (h + 1) * HALF) for h in range(2)]
+
+    with ExitStack() as ctx:
+        keep = ctx.enter_context(tc.tile_pool(name="keep", bufs=1))
+        psum = ctx.enter_context(tc.psum_pool(name="psum", bufs=1))
+
+        def values(name, tag=None):
+            return keep.tile([P, U], F32, name=name, tag=tag or name)
+
+        offs_sb = keep.tile([P, S // 16], U16, name="offs_sb")
+        expy_sb = keep.tile([P, U // 16], U16, name="expy_sb")
+        words = [keep.tile([P, T], I32, name="words%d" % o) for o in range(PASSES)]
+        scale_rows = keep.tile([P, T], U8, name="scale_rows")
+        log_col = keep.tile([P, PACK], F32, name="log_col")
+        mat_col = keep.tile([P, PACK], F32, name="mat_col")
+
+        nc.vector.memset(scale_rows[:].bitcast(I32), 0)
+        nc.scalar.dma_start(out=log_col[:], in_=logfk[0:1, :].rearrange("o (n m) -> (o n) m", m=PACK))
+
+        nc.sync.dma_start(out=words[0][:], in_=x_words[0].rearrange("p n t -> p (n t)").bitcast(I32))
+        nc.sync.dma_start(offs_sb[:], offs)
+        for q in range(4):
+            nc.sync.dma_start(
+                out=scale_rows[32 * q : 32 * q + 4 * PASSES, :].bitcast(I32),
+                in_=x_scales[:, 4 * q : 4 * q + 4, :].bitcast(I32),
+            )
+        nc.sync.dma_start(out=words[1][:], in_=x_words[1].rearrange("p n t -> p (n t)").bitcast(I32))
+        nc.sync.dma_start(out=mat_col[:], in_=mat[0:1, :].rearrange("o (n m) -> (o n) m", m=PACK))
+        raw = {}
+        for name, weight in (("a", w1), ("v", w3)):
+            both = keep.tile([P, PASSES, PACK, N], F32, name="raw_" + name)
+            nc.sync.dma_start(out=both[:], in_=weight.rearrange("(o p j) m -> p o j m", o=PASSES, j=PACK))
+            for o in range(PASSES):
+                raw[name, o] = both[:, o]
+        for o in range(PASSES):
+            one = keep.tile([P, PACK, N], F32, name="raw_r%d" % o)
+            nc.sync.dma_start(out=one[:], in_=w2[o * P * PACK : (o + 1) * P * PACK, :].rearrange("(p j) m -> p j m", j=PACK))
+            raw["r", o] = one[:]
+        nc.sync.dma_start(expy_sb[:], expy)
+        expy_half = [expy_sb[:, h * HALF // 16 : (h + 1) * HALF // 16] for h in range(2)]
+
+        identity = keep.tile([P, P], F32, name="identity")
+        ones = keep.tile([P, P], F32, name="ones")
+        column = keep.tile([P, P], F32, name="column", align_bytes=64)
+        in_quadrant = keep.tile([P, 32], F32, name="in_quadrant", align_bytes=64)
+        quadrant = keep.tile([P, 1], F32, name="quadrant")
+        nc.vector.memset(ones[:], 1.0)
+        for q in range(4):
+            nc.vector.memset(quadrant[32 * q : 32 * (q + 1), :], 32.0 * q)
+        nc.vector.tensor_tensor_scan(column[:], ones[:], ones[:], 0.0, ALU.mult, ALU.add)
+        nc.vector.transpose(in_quadrant[:], column[:, 0:32])
+        nc.vector.tensor_scalar(identity[:], column[:], quadrant[:], in_quadrant[:, 0:1], ALU.subtract, ALU.is_equal)
+        zero = keep.tile([P, 1], F32, name="zero", tag="ln_a")
+        nc.vector.memset(zero[:], 0.0)
+
+        const_col = [keep.tile([P, PACK], F32, name="const_col%d" % c) for c in range(4)]
+        step_col = keep.tile([P, PACK], F32, name="step_col")
+        inv_col = keep.tile([P, PACK], F32, name="inv_col")
+        nc.vector.tensor_scalar(step_col[:], log_col[:], 0.0, 2.0, ALU.is_gt, ALU.mult)
+        nc.vector.reciprocal(inv_col[:], log_col[:])
+        nc.vector.tensor_scalar(const_col[0][:], step_col[:], -1.0, 0.7, ALU.add, ALU.mult)
+        nc.vector.scalar_tensor_tensor(const_col[1][:], const_col[0][:], 5.0 / 2.1, log_col[:], ALU.mult, ALU.mult)
+        nc.vector.scalar_tensor_tensor(const_col[2][:], mat_col[:], 0.0225, inv_col[:], ALU.mult, ALU.mult)
+        nc.vector.scalar_tensor_tensor(const_col[3][:], const_col[2][:], -0.5, inv_col[:], ALU.mult, ALU.mult)
+        spread = []
+        for c in range(4):
+            bank = psum.tile([P, PACK, P], F32, name="spread%d" % c)
+            for m in range(PACK):
+                nc.tensor.transpose(bank[:, m, :], const_col[c][:, m : m + 1].to_broadcast([P, P]), identity[:])
+            spread.append(bank)
+
+        def option_view(ap):
+            return ap.rearrange("p (n m) -> p n m", m=PACK)
+
+        def spread_view(c, h):
+            return spread[c][:, :, h * HALF // PACK : (h + 1) * HALF // PACK].rearrange("p m n -> p n m")
+
+        signed = values("signed")
+        abs_log = values("abs_log")
+        nc.scalar.copy(option_view(signed[:]), spread[0][:].rearrange("p m n -> p n m"))
+        nc.scalar.copy(option_view(abs_log[:]), spread[1][:].rearrange("p m n -> p n m"))
+
+        picked_words = [keep.tile([P, S], U32, name="picked_words%d" % o, align_bytes=64) for o in range(PASSES)]
+        picked_scales = keep.tile([P, S], U8, name="picked_scales", align_bytes=64)
+        nc.vector.tensor_copy(picked_words[0][:], words[0][:].bitcast(U32).indirect(offs_sb[:]))
+        nc.vector.tensor_copy(picked_scales[:], scale_rows[:].indirect(offs_sb[:]))
+        nc.vector.tensor_copy(picked_words[1][:], words[1][:].bitcast(U32).indirect(offs_sb[:]))
+
+        def product(name):
+            acc = psum.tile([P, S], F32, name="acc_" + name)
+            grouped, codes, scales = [], [], []
+            for o in range(PASSES):
+                grouped.append(keep.tile([P, N, PACK], BF16, name="grouped_%s%d" % (name, o), align_bytes=64))
+                codes.append(keep.tile([P, N], U32, name="codes_%s%d" % (name, o), align_bytes=64))
+                scales.append(keep.tile([P, N], U8, name="scales_%s%d" % (name, o), align_bytes=64))
+            first_cast = nc.vector.tensor_copy if name == "r" else nc.scalar.copy
+            first_cast(grouped[0][:], raw[name, 0].rearrange("p j m -> p m j"))
+            nc.vector.tensor_copy(grouped[1][:], raw[name, 1].rearrange("p j m -> p m j"))
+            for o in range(PASSES):
+                nc.vector.quantize_mx(
+                    out=codes[o][:].bitcast(FP8X4), scales=scales[o][:], in_=grouped[o][:].rearrange("p m j -> p (m j)")
+                )
+            for o in range(PASSES):
+                nc.tensor.matmul_mx(
+                    out=acc[:],
+                    lhsT=codes[o][:].bitcast(FP8X4),
+                    lhsT_scale=scales[o][:],
+                    rhs=picked_words[o][:].bitcast(FP8X4),
+                    rhs_scale=picked_scales[4 * o : P, :],
+                    start=(o == 0),
+                    stop=(o == PASSES - 1),
+                )
+            return acc
+
+        ya = product("a")
+        ya_sb = values("ya_sb")
+        nc.scalar.copy(ya_sb[:], ya[:])
+        yv = product("v")
+        abs_v = values("abs_v")
+        exp_v = values("exp_v")
+        nc.scalar.activation(abs_v[:], yv[:], ACT.Abs)
+        nc.scalar.activation(exp_v[:], abs_v[:], ACT.Exp, bias=zero[:], scale=-1.0)
+        yr = product("r")
+        ya_g = values("ya_g")
+        capped = values("capped")
+        exp_a = values("exp_a")
+        for h in range(2):
+            nc.vector.tensor_copy(ya_g[:, halves[h]], ya_sb[:].indirect(expy_half[h]))
+        for h in range(2):
+            nc.vector.tensor_scalar_min(capped[:, halves[h]], ya_g[:, halves[h]], EXP_CAP)
+        tanh_r = values("tanh_r")
+        nc.scalar.activation(tanh_r[:], yr[:], ACT.Tanh, bias=zero[:])
+        for h in range(2):
+            nc.scalar.activation(exp_a[:, halves[h]], capped[:, halves[h]], ACT.Exp, bias=zero[:])
+
+        rho = values("rho")
+        rho_sq = values("rho_sq")
+        curve = values("curve")
+        for h in range(2):
+            nc.vector.tensor_tensor(rho[:, halves[h]], tanh_r[:].indirect(expy_half[h]), signed[:, halves[h]], ALU.mult)
+        for h in range(2):
+            nc.vector.tensor_tensor(rho_sq[:, halves[h]], rho[:, halves[h]], rho[:, halves[h]], ALU.mult)
+        for h in range(2):
+            nc.vector.scalar_tensor_tensor(
+                option_view(curve[:, halves[h]]), option_view(rho_sq[:, halves[h]]), -2.0 / 3.0, spread_view(3, h), ALU.add, ALU.mult
+            )
+
+        ln_a = values("ln_a")
+        ln_v = values("ln_v", tag="exp_a")
+        level = values("level")
+        volvol = values("volvol")
+        reach = values("reach")
+        for h in range(2):
+            nc.scalar.activation(ln_a[:, halves[h]], exp_a[:, halves[h]], ACT.Ln, bias=math.exp(0.3), scale=math.exp(0.3))
+        for h in range(2):
+            nc.scalar.activation(ln_v[:, halves[h]], exp_v[:, halves[h]], ACT.Ln, bias=math.exp(0.2), scale=math.exp(0.2))
+        for h in range(2):
+            nc.vector.scalar_tensor_tensor(level[:, halves[h]], ya_g[:, halves[h]], 0.3, ln_a[:, halves[h]], ALU.add, ALU.max)
+        for h in range(2):
+            nc.vector.scalar_tensor_tensor(volvol[:, halves[h]], yv[:, halves[h]], 0.0, ln_v[:, halves[h]], ALU.max, ALU.add)
+        for h in range(2):
+            nc.vector.tensor_tensor(reach[:, halves[h]], volvol[:].indirect(expy_half[h]), abs_log[:, halves[h]], ALU.mult)
+
+        level_sq = values("level_sq")
+        ln_level = values("ln_level")
+        ln_rest = values("ln_rest", tag="exp_v")
+        reach_sq = values("reach_sq")
+        nc.scalar.activation(level_sq[:], level[:], ACT.Square)
+        nc.scalar.activation(ln_level[:], level[:], ACT.Ln)
+        nc.scalar.activation(ln_rest[:], rho[:], ACT.Ln, bias=1.0, scale=-1.0)
+        for h in range(2):
+            nc.scalar.activation(reach_sq[:, halves[h]], reach[:, halves[h]], ACT.Square)
+
+        tilt = values("tilt")
+        cross = values("cross")
+        squares = values("squares")
+        radicand = values("radicand")
+        root = values("root", tag="rho")
+        shift = values("shift")
+        numer = values("numer")
+        ln_denom = values("ln_denom")
+        ln_numer = values("ln_numer", tag="radicand")
+        for h in range(2):
+            nc.vector.tensor_tensor(tilt[:, halves[h]], rho[:, halves[h]], level[:, halves[h]], ALU.mult)
+        for h in range(2):
+            nc.vector.tensor_tensor(cross[:, halves[h]], tilt[:, halves[h]], reach[:, halves[h]], ALU.mult)
+        for h in range(2):
+            nc.vector.tensor_tensor(squares[:, halves[h]], level_sq[:, halves[h]], reach_sq[:, halves[h]], ALU.add)
+        for h in range(2):
+            nc.vector.scalar_tensor_tensor(radicand[:, halves[h]], cross[:, halves[h]], -2.0, squares[:, halves[h]], ALU.mult, ALU.add)
+        for h in range(2):
+            nc.scalar.activation(root[:, halves[h]], radicand[:, halves[h]], ACT.Sqrt)
+        for h in range(2):
+            nc.vector.tensor_tensor(shift[:, halves[h]], reach[:, halves[h]], tilt[:, halves[h]], ALU.subtract)
+        for h in range(2):
+            nc.vector.tensor_tensor(numer[:, halves[h]], root[:, halves[h]], shift[:, halves[h]], ALU.add)
+        for h in range(2):
+            nc.vector.tensor_tensor(ln_denom[:, halves[h]], ln_level[:, halves[h]], ln_rest[:, halves[h]], ALU.add)
+        for h in range(2):
+            nc.scalar.activation(ln_numer[:, halves[h]], numer[:, halves[h]], ACT.Ln)
+
+        dist = values("dist")
+        ln_dist = values("ln_dist")
+        inv_dist = values("inv_dist", tag="dist")
+        term1 = values("term1")
+        term2 = values("term2")
+        terms = values("terms")
+        scaled = values("scaled")
+        result = values("result")
+        for h in range(2):
+            nc.vector.tensor_tensor(dist[:, halves[h]], ln_numer[:, halves[h]], ln_denom[:, halves[h]], ALU.subtract)
+        for h in range(2):
+            nc.scalar.activation(ln_dist[:, halves[h]], dist[:, halves[h]], ACT.Ln)
+        for h in range(2):
+            nc.scalar.activation(inv_dist[:, halves[h]], ln_dist[:, halves[h]], ACT.Exp, scale=-1.0)
+        for h in range(2):
+            nc.vector.tensor_tensor(option_view(term1[:, halves[h]]), option_view(cross[:, halves[h]]), spread_view(2, h), ALU.mult)
+        for h in range(2):
+            nc.vector.tensor_tensor(term2[:, halves[h]], curve[:, halves[h]], reach_sq[:, halves[h]], ALU.mult)
+        for h in range(2):
+            nc.vector.tensor_tensor(terms[:, halves[h]], term1[:, halves[h]], term2[:, halves[h]], ALU.add)
+        for h in range(2):
+            nc.vector.scalar_tensor_tensor(scaled[:, halves[h]], terms[:, halves[h]], 1.0, reach[:, halves[h]], ALU.add, ALU.mult)
+        for h, queue in enumerate((nc.sync, nc.scalar)):
+            nc.vector.scalar_tensor_tensor(result[:, halves[h]], scaled[:, halves[h]], 1.2, inv_dist[:, halves[h]], ALU.mult, ALU.mult)
+            queue.dma_start(out=out[:, halves[h]], in_=result[:, halves[h]])

@@ -27,6 +27,8 @@ def tile_picked_ysabr_vol_p_kernel(tc, x_words, x_scales, w1, w2, w3, logfk, mat
     nc = tc.nc
     halves = [slice(h * HALF, (h + 1) * HALF) for h in range(2)]
 
+    quarters = [slice(q * U // 4, (q + 1) * U // 4) for q in range(4)]
+
     with ExitStack() as ctx:
         keep = ctx.enter_context(tc.tile_pool(name="keep", bufs=1))
         psum = ctx.enter_context(tc.psum_pool(name="psum", bufs=1))
@@ -160,94 +162,87 @@ def tile_picked_ysabr_vol_p_kernel(tc, x_words, x_scales, w1, w2, w3, logfk, mat
         for h in range(2):
             nc.scalar.activation(exp_a[:, halves[h]], capped[:, halves[h]], ACT.Exp, bias=zero[:])
 
-        rho = values("rho")
-        rho_sq = values("rho_sq")
-        curve = values("curve")
+        rho = values("rho", tag="ya_sb")
         for h in range(2):
             nc.vector.tensor_tensor(rho[:, halves[h]], tanh_r[:].indirect(expy_half[h]), signed[:, halves[h]], ALU.mult)
-        for h in range(2):
-            nc.vector.tensor_tensor(rho_sq[:, halves[h]], rho[:, halves[h]], rho[:, halves[h]], ALU.mult)
+
+        def vector_step(op, result, left, right, scalar=None, scalar_op=None, pieces=halves):
+            for cols in pieces:
+                if scalar is None:
+                    nc.vector.tensor_tensor(result[:, cols], left[:, cols], right[:, cols], op)
+                else:
+                    nc.vector.scalar_tensor_tensor(result[:, cols], left[:, cols], scalar, right[:, cols], scalar_op, op)
+
+        def scalar_step(func, result, source, pieces=halves, **affine):
+            for cols in pieces:
+                nc.scalar.activation(result[:, cols], source[:, cols], func, **affine)
+
+        rho_sq = values("rho_sq")
+        curve = values("curve")
+        vector_step(ALU.mult, rho_sq, rho, rho)
         for h in range(2):
             nc.vector.scalar_tensor_tensor(
                 option_view(curve[:, halves[h]]), option_view(rho_sq[:, halves[h]]), -2.0 / 3.0, spread_view(3, h), ALU.add, ALU.mult
             )
 
-        ln_a = values("ln_a")
-        ln_v = values("ln_v", tag="exp_a")
+        logs = keep.tile([P, 3, U], F32, name="logs", tag="ln_a")
+        ln_a, ln_v, ln_rest = logs[:, 0, :], logs[:, 1, :], logs[:, 2, :]
         level = values("level")
         volvol = values("volvol")
+        tilt = values("tilt")
         reach = values("reach")
-        for h in range(2):
-            nc.scalar.activation(ln_a[:, halves[h]], exp_a[:, halves[h]], ACT.Ln, bias=math.exp(0.3), scale=math.exp(0.3))
-        for h in range(2):
-            nc.scalar.activation(ln_v[:, halves[h]], exp_v[:, halves[h]], ACT.Ln, bias=math.exp(0.2), scale=math.exp(0.2))
-        for h in range(2):
-            nc.vector.scalar_tensor_tensor(level[:, halves[h]], ya_g[:, halves[h]], 0.3, ln_a[:, halves[h]], ALU.add, ALU.max)
-        for h in range(2):
-            nc.vector.scalar_tensor_tensor(volvol[:, halves[h]], yv[:, halves[h]], 0.0, ln_v[:, halves[h]], ALU.max, ALU.add)
-        for h in range(2):
-            nc.vector.tensor_tensor(reach[:, halves[h]], volvol[:].indirect(expy_half[h]), abs_log[:, halves[h]], ALU.mult)
-
         level_sq = values("level_sq")
         ln_level = values("ln_level")
-        ln_rest = values("ln_rest", tag="exp_v")
-        reach_sq = values("reach_sq")
+        scalar_step(ACT.Ln, ln_a, exp_a, bias=math.exp(0.3), scale=math.exp(0.3))
+        scalar_step(ACT.Ln, ln_v, exp_v, bias=math.exp(0.2), scale=math.exp(0.2))
+        vector_step(ALU.max, level, ya_g, ln_a, 0.3, ALU.add)
+        vector_step(ALU.add, volvol, yv, ln_v, 0.0, ALU.max)
+        vector_step(ALU.mult, tilt, rho, level)
+        for h in range(2):
+            nc.vector.tensor_tensor(reach[:, halves[h]], volvol[:].indirect(expy_half[h]), abs_log[:, halves[h]], ALU.mult)
+        nc.scalar.activation(ln_rest, rho[:], ACT.Ln, bias=1.0, scale=-1.0)
         nc.scalar.activation(level_sq[:], level[:], ACT.Square)
-        nc.scalar.activation(ln_level[:], level[:], ACT.Ln)
-        nc.scalar.activation(ln_rest[:], rho[:], ACT.Ln, bias=1.0, scale=-1.0)
-        for h in range(2):
-            nc.scalar.activation(reach_sq[:, halves[h]], reach[:, halves[h]], ACT.Square)
+        scalar_step(ACT.Ln, ln_level, level)
 
-        tilt = values("tilt")
+        table_warm = keep.tile([P, 3], F32, name="table_warm")
+        reach_sq = values("reach_sq")
         cross = values("cross")
-        squares = values("squares")
+        partial = values("partial")
         radicand = values("radicand")
-        root = values("root", tag="rho")
-        shift = values("shift")
+        root = values("root")
+        later = keep.tile([P, 3, U], F32, name="later", tag="partial")
+        shift, ln_denom, term1 = (later[:, i, :] for i in range(3))
         numer = values("numer")
-        ln_denom = values("ln_denom")
-        ln_numer = values("ln_numer", tag="radicand")
-        for h in range(2):
-            nc.vector.tensor_tensor(tilt[:, halves[h]], rho[:, halves[h]], level[:, halves[h]], ALU.mult)
-        for h in range(2):
-            nc.vector.tensor_tensor(cross[:, halves[h]], tilt[:, halves[h]], reach[:, halves[h]], ALU.mult)
-        for h in range(2):
-            nc.vector.tensor_tensor(squares[:, halves[h]], level_sq[:, halves[h]], reach_sq[:, halves[h]], ALU.add)
-        for h in range(2):
-            nc.vector.scalar_tensor_tensor(radicand[:, halves[h]], cross[:, halves[h]], -2.0, squares[:, halves[h]], ALU.mult, ALU.add)
-        for h in range(2):
-            nc.scalar.activation(root[:, halves[h]], radicand[:, halves[h]], ACT.Sqrt)
-        for h in range(2):
-            nc.vector.tensor_tensor(shift[:, halves[h]], reach[:, halves[h]], tilt[:, halves[h]], ALU.subtract)
-        for h in range(2):
-            nc.vector.tensor_tensor(numer[:, halves[h]], root[:, halves[h]], shift[:, halves[h]], ALU.add)
-        for h in range(2):
-            nc.vector.tensor_tensor(ln_denom[:, halves[h]], ln_level[:, halves[h]], ln_rest[:, halves[h]], ALU.add)
-        for h in range(2):
-            nc.scalar.activation(ln_numer[:, halves[h]], numer[:, halves[h]], ACT.Ln)
+        nc.scalar.activation(table_warm[:, 0:1], ln_level[:, 0:1], ACT.Sqrt, bias=1.0, scale=0.0)
+        scalar_step(ACT.Square, reach_sq, reach)
+        vector_step(ALU.mult, cross, tilt, reach)
+        vector_step(ALU.add, partial, cross, level_sq, -2.0, ALU.mult)
+        vector_step(ALU.add, radicand, partial, reach_sq)
+        scalar_step(ACT.Sqrt, root, radicand)
+        nc.scalar.activation(table_warm[:, 1:2], root[:, 0:1], ACT.Ln)
+        vector_step(ALU.subtract, shift, reach, tilt)
+        vector_step(ALU.add, numer, root, shift)
+        vector_step(ALU.add, ln_denom, ln_level, ln_rest)
 
+        ln_numer = values("ln_numer")
         dist = values("dist")
         ln_dist = values("ln_dist")
         inv_dist = values("inv_dist", tag="dist")
-        term1 = values("term1")
-        term2 = values("term2")
+        scalar_step(ACT.Ln, ln_numer, numer, pieces=quarters)
+        vector_step(ALU.subtract, dist, ln_numer, ln_denom, pieces=quarters)
+        scalar_step(ACT.Ln, ln_dist, dist, pieces=quarters)
+        scalar_step(ACT.Exp, inv_dist, ln_dist, pieces=quarters, scale=-1.0)
+
+        term2 = values("term2", tag="ln_numer")
         terms = values("terms")
         scaled = values("scaled")
         result = values("result")
         for h in range(2):
-            nc.vector.tensor_tensor(dist[:, halves[h]], ln_numer[:, halves[h]], ln_denom[:, halves[h]], ALU.subtract)
-        for h in range(2):
-            nc.scalar.activation(ln_dist[:, halves[h]], dist[:, halves[h]], ACT.Ln)
-        for h in range(2):
-            nc.scalar.activation(inv_dist[:, halves[h]], ln_dist[:, halves[h]], ACT.Exp, scale=-1.0)
-        for h in range(2):
             nc.vector.tensor_tensor(option_view(term1[:, halves[h]]), option_view(cross[:, halves[h]]), spread_view(2, h), ALU.mult)
-        for h in range(2):
-            nc.vector.tensor_tensor(term2[:, halves[h]], curve[:, halves[h]], reach_sq[:, halves[h]], ALU.mult)
-        for h in range(2):
-            nc.vector.tensor_tensor(terms[:, halves[h]], term1[:, halves[h]], term2[:, halves[h]], ALU.add)
-        for h in range(2):
-            nc.vector.scalar_tensor_tensor(scaled[:, halves[h]], terms[:, halves[h]], 1.0, reach[:, halves[h]], ALU.add, ALU.mult)
-        for h, queue in enumerate((nc.sync, nc.scalar)):
-            nc.vector.scalar_tensor_tensor(result[:, halves[h]], scaled[:, halves[h]], 1.2, inv_dist[:, halves[h]], ALU.mult, ALU.mult)
-            queue.dma_start(out=out[:, halves[h]], in_=result[:, halves[h]])
+        vector_step(ALU.mult, term2, curve, reach_sq)
+        vector_step(ALU.add, terms, term1, term2)
+        vector_step(ALU.mult, scaled, terms, reach, 1.0, ALU.add)
+        for cols in quarters:
+            nc.vector.scalar_tensor_tensor(result[:, cols], scaled[:, cols], 1.2, inv_dist[:, cols], ALU.mult, ALU.mult)
+            queue = nc.scalar if cols is quarters[-1] else nc.sync
+            queue.dma_start(out=out[:, cols], in_=result[:, cols])

@@ -93,21 +93,15 @@ def tile_picked_ysabr_vol_p_kernel(tc, x_words, x_scales, w1, w2, w3, logfk, mat
         nc.vector.scalar_tensor_tensor(const_col[3][:], const_col[2][:], -0.5, inv_col[:], ALU.mult, ALU.mult)
         spread = []
         for c in range(4):
-            bank = psum.tile([P, PACK, P], F32, name="spread%d" % c)
+            bank = psum.tile([P, U], F32, name="spread%d" % c)
             for m in range(PACK):
-                nc.tensor.transpose(bank[:, m, :], const_col[c][:, m : m + 1].to_broadcast([P, P]), identity[:])
+                nc.tensor.transpose(bank[:, m::PACK], const_col[c][:, m : m + 1].to_broadcast([P, P]), identity[:])
             spread.append(bank)
-
-        def option_view(ap):
-            return ap.rearrange("p (n m) -> p n m", m=PACK)
-
-        def spread_view(c, h):
-            return spread[c][:, :, h * HALF // PACK : (h + 1) * HALF // PACK].rearrange("p m n -> p n m")
 
         signed = values("signed")
         abs_log = values("abs_log")
-        nc.scalar.copy(option_view(signed[:]), spread[0][:].rearrange("p m n -> p n m"))
-        nc.scalar.copy(option_view(abs_log[:]), spread[1][:].rearrange("p m n -> p n m"))
+        nc.scalar.copy(signed[:], spread[0][:])
+        nc.scalar.copy(abs_log[:], spread[1][:])
 
         picked_words = [keep.tile([P, S], U32, name="picked_words%d" % o, align_bytes=64) for o in range(PASSES)]
         picked_scales = keep.tile([P, S], U8, name="picked_scales", align_bytes=64)
@@ -122,9 +116,9 @@ def tile_picked_ysabr_vol_p_kernel(tc, x_words, x_scales, w1, w2, w3, logfk, mat
                 grouped.append(keep.tile([P, N, PACK], BF16, name="grouped_%s%d" % (name, o), align_bytes=64))
                 codes.append(keep.tile([P, N], U32, name="codes_%s%d" % (name, o), align_bytes=64))
                 scales.append(keep.tile([P, N], U8, name="scales_%s%d" % (name, o), align_bytes=64))
-            first_cast = nc.vector.tensor_copy if name == "r" else nc.scalar.copy
-            first_cast(grouped[0][:], raw[name, 0].rearrange("p j m -> p m j"))
-            nc.vector.tensor_copy(grouped[1][:], raw[name, 1].rearrange("p j m -> p m j"))
+            second_cast = nc.vector.tensor_copy if name == "r" else nc.scalar.copy
+            nc.vector.tensor_copy(grouped[0][:], raw[name, 0].rearrange("p j m -> p m j"))
+            second_cast(grouped[1][:], raw[name, 1].rearrange("p j m -> p m j"))
             for o in range(PASSES):
                 nc.vector.quantize_mx(
                     out=codes[o][:].bitcast(FP8X4), scales=scales[o][:], in_=grouped[o][:].rearrange("p m j -> p (m j)")
@@ -180,10 +174,7 @@ def tile_picked_ysabr_vol_p_kernel(tc, x_words, x_scales, w1, w2, w3, logfk, mat
         rho_sq = values("rho_sq")
         curve = values("curve")
         vector_step(ALU.mult, rho_sq, rho, rho)
-        for h in range(2):
-            nc.vector.scalar_tensor_tensor(
-                option_view(curve[:, halves[h]]), option_view(rho_sq[:, halves[h]]), -2.0 / 3.0, spread_view(3, h), ALU.add, ALU.mult
-            )
+        vector_step(ALU.mult, curve, rho_sq, spread[3], -2.0 / 3.0, ALU.add)
 
         logs = keep.tile([P, 3, U], F32, name="logs", tag="ln_a")
         ln_a, ln_v, ln_rest = logs[:, 0, :], logs[:, 1, :], logs[:, 2, :]
@@ -210,8 +201,8 @@ def tile_picked_ysabr_vol_p_kernel(tc, x_words, x_scales, w1, w2, w3, logfk, mat
         partial = values("partial")
         radicand = values("radicand")
         root = values("root")
-        later = keep.tile([P, 3, U], F32, name="later", tag="partial")
-        shift, ln_denom, term1 = (later[:, i, :] for i in range(3))
+        later = keep.tile([P, 4, U], F32, name="later", tag="partial")
+        shift, ln_denom, term1, term2 = (later[:, i, :] for i in range(4))
         numer = values("numer")
         nc.scalar.activation(table_warm[:, 0:1], ln_level[:, 0:1], ACT.Sqrt, bias=1.0, scale=0.0)
         scalar_step(ACT.Square, reach_sq, reach)
@@ -225,24 +216,26 @@ def tile_picked_ysabr_vol_p_kernel(tc, x_words, x_scales, w1, w2, w3, logfk, mat
         vector_step(ALU.add, ln_denom, ln_level, ln_rest)
 
         ln_numer = values("ln_numer")
+        dist_first = keep.tile([P, U // 4], F32, name="dist_first")
         dist = values("dist")
         ln_dist = values("ln_dist")
+        inv_first = keep.tile([P, U // 4], F32, name="inv_first")
         inv_dist = values("inv_dist", tag="dist")
         scalar_step(ACT.Ln, ln_numer, numer, pieces=quarters)
-        vector_step(ALU.subtract, dist, ln_numer, ln_denom, pieces=quarters)
-        scalar_step(ACT.Ln, ln_dist, dist, pieces=quarters)
-        scalar_step(ACT.Exp, inv_dist, ln_dist, pieces=quarters, scale=-1.0)
+        vector_step(ALU.subtract, dist, ln_numer, ln_denom, pieces=quarters[:3])
+        nc.vector.tensor_tensor(dist_first[:], ln_numer[:, quarters[3]], ln_denom[:, quarters[3]], ALU.subtract)
+        nc.vector.reciprocal(inv_first[:], dist_first[:])
+        scalar_step(ACT.Ln, ln_dist, dist, pieces=quarters[:3])
+        scalar_step(ACT.Exp, inv_dist, ln_dist, pieces=quarters[:3], scale=-1.0)
 
-        term2 = values("term2", tag="ln_numer")
         terms = values("terms")
         scaled = values("scaled")
         result = values("result")
-        for h in range(2):
-            nc.vector.tensor_tensor(option_view(term1[:, halves[h]]), option_view(cross[:, halves[h]]), spread_view(2, h), ALU.mult)
+        vector_step(ALU.mult, term1, cross, spread[2])
         vector_step(ALU.mult, term2, curve, reach_sq)
         vector_step(ALU.add, terms, term1, term2)
         vector_step(ALU.mult, scaled, terms, reach, 1.0, ALU.add)
-        for cols in quarters:
-            nc.vector.scalar_tensor_tensor(result[:, cols], scaled[:, cols], 1.2, inv_dist[:, cols], ALU.mult, ALU.mult)
-            queue = nc.scalar if cols is quarters[-1] else nc.sync
+        for cols in quarters[3:] + quarters[:3]:
+            nc.vector.scalar_tensor_tensor(result[:, cols], scaled[:, cols], 1.2, inv_first[:] if cols is quarters[3] else inv_dist[:, cols], ALU.mult, ALU.mult)
+            queue = nc.scalar if cols is quarters[2] else nc.sync
             queue.dma_start(out=out[:, cols], in_=result[:, cols])

import math
from contextlib import ExitStack

import concourse.mybir as mybir

K, T, S, N, U = 1024, 2048, 512, 128, 512
FLOPS = 3 * 2 * K * N * S

F32 = mybir.dt.float32
BF16 = mybir.dt.bfloat16
I32 = mybir.dt.int32
U32 = mybir.dt.uint32
U16 = mybir.dt.uint16
U8 = mybir.dt.uint8
FP8X4 = mybir.dt.float8_e4m3fn_x4
ALU = mybir.AluOpType
ACT = mybir.ActivationFunctionType

P = 128
PACK = 4
PASSES = K // (P * PACK)
HALF = U // 2
EXP_CAP = 30.0


def tile_picked_ysabr_vol_p_kernel(tc, x_words, x_scales, w1, w2, w3, logfk, mat, offs, expy, out):
    nc = tc.nc
    halves = [slice(h * HALF, (h + 1) * HALF) for h in range(2)]

    quarters = [slice(q * U // 4, (q + 1) * U // 4) for q in range(4)]

    with ExitStack() as ctx:
        keep = ctx.enter_context(tc.tile_pool(name="keep", bufs=1))
        psum = ctx.enter_context(tc.psum_pool(name="psum", bufs=1))

        def values(name, tag=None):
            return keep.tile([P, U], F32, name=name, tag=tag or name)

        offs_sb = keep.tile([P, S // 16], U16, name="offs_sb")
        expy_sb = keep.tile([P, U // 16], U16, name="expy_sb")
        words = [keep.tile([P, T], I32, name="words%d" % o) for o in range(PASSES)]
        scale_rows = keep.tile([P, T], U8, name="scale_rows")
        log_col = keep.tile([P, PACK], F32, name="log_col")
        mat_col = keep.tile([P, PACK], F32, name="mat_col")

        nc.vector.memset(scale_rows[:].bitcast(I32), 0)
        nc.scalar.dma_start(out=log_col[:], in_=logfk[0:1, :].rearrange("o (n m) -> (o n) m", m=PACK))

        nc.sync.dma_start(out=words[0][:], in_=x_words[0].rearrange("p n t -> p (n t)").bitcast(I32))
        nc.sync.dma_start(offs_sb[:], offs)
        for q in range(4):
            nc.sync.dma_start(
                out=scale_rows[32 * q : 32 * q + 4 * PASSES, :].bitcast(I32),
                in_=x_scales[:, 4 * q : 4 * q + 4, :].bitcast(I32),
            )
        nc.sync.dma_start(out=words[1][:], in_=x_words[1].rearrange("p n t -> p (n t)").bitcast(I32))
        nc.sync.dma_start(out=mat_col[:], in_=mat[0:1, :].rearrange("o (n m) -> (o n) m", m=PACK))
        raw = {}
        for name, weight in (("a", w1), ("v", w3)):
            both = keep.tile([P, PASSES, PACK, N], F32, name="raw_" + name)
            nc.sync.dma_start(out=both[:], in_=weight.rearrange("(o p j) m -> p o j m", o=PASSES, j=PACK))
            for o in range(PASSES):
                raw[name, o] = both[:, o]
        for o in range(PASSES):
            one = keep.tile([P, PACK, N], F32, name="raw_r%d" % o)
            nc.sync.dma_start(out=one[:], in_=w2[o * P * PACK : (o + 1) * P * PACK, :].rearrange("(p j) m -> p j m", j=PACK))
            raw["r", o] = one[:]
        nc.sync.dma_start(expy_sb[:], expy)
        expy_half = [expy_sb[:, h * HALF // 16 : (h + 1) * HALF // 16] for h in range(2)]

        identity = keep.tile([P, P], F32, name="identity")
        ones = keep.tile([P, P], F32, name="ones")
        column = keep.tile([P, P], F32, name="column", align_bytes=64)
        in_quadrant = keep.tile([P, 32], F32, name="in_quadrant", align_bytes=64)
        quadrant = keep.tile([P, 1], F32, name="quadrant")
        nc.vector.memset(ones[:], 1.0)
        for q in range(4):
            nc.vector.memset(quadrant[32 * q : 32 * (q + 1), :], 32.0 * q)
        nc.vector.tensor_tensor_scan(column[:], ones[:], ones[:], 0.0, ALU.mult, ALU.add)
        nc.vector.transpose(in_quadrant[:], column[:, 0:32])
        nc.vector.tensor_scalar(identity[:], column[:], quadrant[:], in_quadrant[:, 0:1], ALU.subtract, ALU.is_equal)
        zero = keep.tile([P, 1], F32, name="zero", tag="ln_a")
        nc.vector.memset(zero[:], 0.0)

        const_col = [keep.tile([P, PACK], F32, name="const_col%d" % c) for c in range(4)]
        step_col = keep.tile([P, PACK], F32, name="step_col")
        inv_col = keep.tile([P, PACK], F32, name="inv_col")
        nc.vector.tensor_scalar(step_col[:], log_col[:], 0.0, 2.0, ALU.is_gt, ALU.mult)
        nc.vector.reciprocal(inv_col[:], log_col[:])
        nc.vector.tensor_scalar(const_col[0][:], step_col[:], -1.0, 0.7, ALU.add, ALU.mult)
        nc.vector.scalar_tensor_tensor(const_col[1][:], const_col[0][:], 5.0 / 2.1, log_col[:], ALU.mult, ALU.mult)
        nc.vector.scalar_tensor_tensor(const_col[2][:], mat_col[:], 0.0225, inv_col[:], ALU.mult, ALU.mult)
        nc.vector.scalar_tensor_tensor(const_col[3][:], const_col[2][:], -0.5, inv_col[:], ALU.mult, ALU.mult)
        spread = []
        for c in range(4):
            bank = psum.tile([P, U], F32, name="spread%d" % c)
            for m in range(PACK):
                nc.tensor.transpose(bank[:, m::PACK], const_col[c][:, m : m + 1].to_broadcast([P, P]), identity[:])
            spread.append(bank)

        signed = values("signed")
        abs_log = values("abs_log")
        nc.scalar.copy(signed[:], spread[0][:])
        nc.scalar.copy(abs_log[:], spread[1][:])

        picked_words = [keep.tile([P, S], U32, name="picked_words%d" % o, align_bytes=64) for o in range(PASSES)]
        picked_scales = keep.tile([P, S], U8, name="picked_scales", align_bytes=64)
        nc.vector.tensor_copy(picked_words[0][:], words[0][:].bitcast(U32).indirect(offs_sb[:]))
        nc.vector.tensor_copy(picked_scales[:], scale_rows[:].indirect(offs_sb[:]))
        nc.vector.tensor_copy(picked_words[1][:], words[1][:].bitcast(U32).indirect(offs_sb[:]))

        def product(name):
            acc = psum.tile([P, S], F32, name="acc_" + name)
            grouped, codes, scales = [], [], []
            for o in range(PASSES):
                grouped.append(keep.tile([P, N, PACK], BF16, name="grouped_%s%d" % (name, o), align_bytes=64))
                codes.append(keep.tile([P, N], U32, name="codes_%s%d" % (name, o), align_bytes=64))
                scales.append(keep.tile([P, N], U8, name="scales_%s%d" % (name, o), align_bytes=64))
            second_cast = nc.vector.tensor_copy if name == "r" else nc.scalar.copy
            nc.vector.tensor_copy(grouped[0][:], raw[name, 0].rearrange("p j m -> p m j"))
            second_cast(grouped[1][:], raw[name, 1].rearrange("p j m -> p m j"))
            for o in range(PASSES):
                nc.vector.quantize_mx(
                    out=codes[o][:].bitcast(FP8X4), scales=scales[o][:], in_=grouped[o][:].rearrange("p m j -> p (m j)")
                )
            for o in range(PASSES):
                nc.tensor.matmul_mx(
                    out=acc[:],
                    lhsT=codes[o][:].bitcast(FP8X4),
                    lhsT_scale=scales[o][:],
                    rhs=picked_words[o][:].bitcast(FP8X4),
                    rhs_scale=picked_scales[4 * o : P, :],
                    start=(o == 0),
                    stop=(o == PASSES - 1),
                )
            return acc

        ya = product("a")
        ya_sb = values("ya_sb")
        nc.scalar.copy(ya_sb[:], ya[:])
        yv = product("v")
        abs_v = values("abs_v")
        exp_v = values("exp_v")
        nc.scalar.activation(abs_v[:], yv[:], ACT.Abs)
        nc.scalar.activation(exp_v[:], abs_v[:], ACT.Exp, bias=zero[:], scale=-1.0)
        yr = product("r")
        ya_g = values("ya_g")
        capped = values("capped")
        exp_a = values("exp_a")
        for h in range(2):
            nc.vector.tensor_copy(ya_g[:, halves[h]], ya_sb[:].indirect(expy_half[h]))
        for h in range(2):
            nc.vector.tensor_scalar_min(capped[:, halves[h]], ya_g[:, halves[h]], EXP_CAP)
        tanh_r = values("tanh_r")
        nc.scalar.activation(tanh_r[:], yr[:], ACT.Tanh, bias=zero[:])
        for h in range(2):
            nc.scalar.activation(exp_a[:, halves[h]], capped[:, halves[h]], ACT.Exp, bias=zero[:])

        rho = values("rho", tag="ya_sb")
        for h in range(2):
            nc.vector.tensor_tensor(rho[:, halves[h]], tanh_r[:].indirect(expy_half[h]), signed[:, halves[h]], ALU.mult)

        def vector_step(op, result, left, right, scalar=None, scalar_op=None, pieces=halves):
            for cols in pieces:
                if scalar is None:
                    nc.vector.tensor_tensor(result[:, cols], left[:, cols], right[:, cols], op)
                else:
                    nc.vector.scalar_tensor_tensor(result[:, cols], left[:, cols], scalar, right[:, cols], scalar_op, op)

        def scalar_step(func, result, source, pieces=halves, **affine):
            for cols in pieces:
                nc.scalar.activation(result[:, cols], source[:, cols], func, **affine)

        rho_sq = values("rho_sq")
        curve = values("curve")
        vector_step(ALU.mult, rho_sq, rho, rho)
        vector_step(ALU.mult, curve, rho_sq, spread[3], -2.0 / 3.0, ALU.add)

        logs = keep.tile([P, 3, U], F32, name="logs", tag="ln_a")
        ln_a, ln_v, ln_rest = logs[:, 0, :], logs[:, 1, :], logs[:, 2, :]
        level = values("level")
        volvol = values("volvol")
        tilt = values("tilt")
        reach = values("reach")
        level_sq = values("level_sq")
        ln_level = values("ln_level")
        scalar_step(ACT.Ln, ln_a, exp_a, bias=math.exp(0.3), scale=math.exp(0.3))
        scalar_step(ACT.Ln, ln_v, exp_v, bias=math.exp(0.2), scale=math.exp(0.2))
        vector_step(ALU.max, level, ya_g, ln_a, 0.3, ALU.add)
        vector_step(ALU.add, volvol, yv, ln_v, 0.0, ALU.max)
        vector_step(ALU.mult, tilt, rho, level)
        for h in range(2):
            nc.vector.tensor_tensor(reach[:, halves[h]], volvol[:].indirect(expy_half[h]), abs_log[:, halves[h]], ALU.mult)
        nc.scalar.activation(ln_rest, rho[:], ACT.Ln, bias=1.0, scale=-1.0)
        nc.scalar.activation(level_sq[:], level[:], ACT.Square)
        scalar_step(ACT.Ln, ln_level, level)

        table_warm = keep.tile([P, 3], F32, name="table_warm")
        reach_sq = values("reach_sq")
        cross = values("cross")
        partial = values("partial")
        radicand = values("radicand")
        root = values("root")
        later = keep.tile([P, 4, U], F32, name="later", tag="partial")
        shift, ln_denom, term1, term2 = (later[:, i, :] for i in range(4))
        numer = values("numer")
        nc.scalar.activation(table_warm[:, 0:1], ln_level[:, 0:1], ACT.Sqrt, bias=1.0, scale=0.0)
        scalar_step(ACT.Square, reach_sq, reach)
        vector_step(ALU.mult, cross, tilt, reach)
        vector_step(ALU.add, partial, cross, level_sq, -2.0, ALU.mult)
        vector_step(ALU.add, radicand, partial, reach_sq)
        scalar_step(ACT.Sqrt, root, radicand)
        nc.scalar.activation(table_warm[:, 1:2], root[:, 0:1], ACT.Ln)
        vector_step(ALU.subtract, shift, reach, tilt)
        vector_step(ALU.add, numer, root, shift)
        vector_step(ALU.add, ln_denom, ln_level, ln_rest)

        ln_numer = values("ln_numer")
        dist_first = keep.tile([P, U // 4], F32, name="dist_first")
        dist = values("dist")
        ln_dist = values("ln_dist")
        inv_first = keep.tile([P, U // 4], F32, name="inv_first")
        inv_dist = values("inv_dist", tag="dist")
        scalar_step(ACT.Ln, ln_numer, numer, pieces=quarters)
        vector_step(ALU.subtract, dist, ln_numer, ln_denom, pieces=quarters[:3])
        nc.vector.tensor_tensor(dist_first[:], ln_numer[:, quarters[3]], ln_denom[:, quarters[3]], ALU.subtract)
        nc.vector.reciprocal(inv_first[:], dist_first[:])
        scalar_step(ACT.Ln, ln_dist, dist, pieces=quarters[:3])
        scalar_step(ACT.Exp, inv_dist, ln_dist, pieces=quarters[:3], scale=-1.0)

        terms = values("terms")
        scaled = values("scaled")
        result = values("result")
        vector_step(ALU.mult, term1, cross, spread[2])
        vector_step(ALU.mult, term2, curve, reach_sq)
        vector_step(ALU.add, terms, term1, term2)
        vector_step(ALU.mult, scaled, terms, reach, 1.0, ALU.add)
        for cols in quarters[3:] + quarters[:3]:
            nc.vector.scalar_tensor_tensor(result[:, cols], scaled[:, cols], 1.2, inv_first[:] if cols is quarters[3] else inv_dist[:, cols], ALU.mult, ALU.mult)
            queue = nc.scalar if cols is quarters[2] else nc.sync
            queue.dma_start(out=out[:, cols], in_=result[:, cols])
